import numpy as np
import ml_dtypes


def mxq(x, axis, fmt="e4m3"):
    dtype, down = {"e4m3": (ml_dtypes.float8_e4m3fn, 7), "e5m2": (ml_dtypes.float8_e5m2, 14)}[fmt]
    v = np.moveaxis(np.asarray(x, np.float32).astype(ml_dtypes.bfloat16).astype(np.float64), axis, -1)
    blocks = v.reshape(v.shape[:-1] + (-1, 32))
    amax = np.abs(blocks).max(-1, keepdims=True)
    byte = np.maximum(np.where(amax > 0, np.frexp(amax)[1] - 1 + 127, 0) - down, 1)
    scale = np.exp2(byte - 127.0)
    codes = (blocks / scale).astype(np.float32).astype(dtype).astype(np.float64)
    return np.moveaxis((codes * scale).reshape(v.shape), -1, axis)


WIDE = False


def mx_kscale(k):
    if not WIDE:
        return np.ones(k)
    levels = np.array([30, -30])
    if k % 512:
        return np.exp2(np.random.permutation(np.resize(levels, k // 32))).repeat(32)
    a = np.empty((k // 512, 16))
    for p in range(k // 512):
        a[p, :8] = np.random.permutation(np.resize(levels, 8))
        for g in range(8):
            far = levels[np.abs(levels - a[p, g]) >= 10]
            a[p, g + 8] = far[np.random.randint(len(far))]
    return np.exp2(a.ravel()).repeat(32)


BF16 = ml_dtypes.bfloat16


def bf(x):
    return np.asarray(x, np.float32).astype(BF16)


def f64(x):
    return np.asarray(x).astype(np.float64)


E2M1 = np.array([0.0, 0.5, 1.0, 1.5, 2.0, 3.0, 4.0, 6.0, -0.0, -0.5, -1.0, -1.5, -2.0, -3.0, -4.0, -6.0])


def pack_weight(w, fmt):
    k, n = w.shape
    w = f64(bf(w)).reshape(k // 32, 32, n)
    amax = np.abs(w).max(1)
    if fmt in ("e4m3", "e5m2"):
        byte = np.frexp(amax)[1] - 1 + 127 - (7 if fmt == "e4m3" else 14)
    else:
        mant, ex = np.frexp(amax / 6.0)
        byte = np.where(mant > 0.5, ex, ex - 1) + 127
    byte = np.clip(np.where(amax > 0, byte, 1), 1, 254)
    scaled = (w * np.exp2(127.0 - byte)[:, None, :]).reshape(k, n).astype(np.float32)
    by_word = np.ascontiguousarray(scaled.reshape(k // 512, 128, 4, n).transpose(0, 1, 3, 2))
    if fmt in ("e4m3", "e5m2"):
        words = by_word.astype(ml_dtypes.float8_e4m3fn if fmt == "e4m3" else ml_dtypes.float8_e5m2).view(np.uint8)
    else:
        c = by_word.astype(ml_dtypes.float4_e2m1fn).view(np.uint8) & 0xF
        words = c[..., 0::2] | (c[..., 1::2] << 4)
    return np.ascontiguousarray(words), np.ascontiguousarray(byte.astype(np.uint8).reshape(k // 512, 16, n))


def unpack_weight(words, scales, fmt):
    g, p, n, _ = words.shape
    if fmt in ("e4m3", "e5m2"):
        vals = np.ascontiguousarray(words).view(ml_dtypes.float8_e4m3fn if fmt == "e4m3" else ml_dtypes.float8_e5m2).astype(np.float64)
    else:
        nib = np.empty((g, p, n, 4), np.uint8)
        nib[..., 0::2] = words & 0xF
        nib[..., 1::2] = words >> 4
        vals = E2M1[nib]
    vals = vals * np.repeat(np.exp2(scales.astype(np.float64) - 127.0), 8, axis=1)[..., None]
    return vals.transpose(0, 1, 3, 2).reshape(g * 512, n)


I, J, L, R = 2048, 128, 32, 512


def setup_inputs():
    s = mx_kscale(J * L)
    G = np.random.standard_normal((J * L, I)) * np.exp(0.5 * np.random.standard_normal((J * L, I)))
    g_words, g_scales = pack_weight(G / s[:, None], "e5m2")
    return {"g_words": g_words, "g_scales": g_scales,
            "b": bf(np.random.standard_normal((J, R)) / np.sqrt(J) * s.reshape(J, L)[:, :1]),
            "c": bf(np.random.standard_normal((L, R)) / np.sqrt(L)),
            "a": bf(np.random.standard_normal((I, R))),
            "weight": bf(1 + 0.1 * np.random.standard_normal(R)),
            "ridge": bf(np.random.uniform(0.2, 0.5, R))}


def reference(g_words, g_scales, b, c, a, weight, ridge):
    G = unpack_weight(g_words, g_scales, "e5m2")
    kr = (f64(b)[:, None, :] * f64(c)[None, :, :]).reshape(J * L, R)
    m = G.T @ mxq(kr, 0, "e4m3")
    return m * f64(weight) + f64(a) * f64(ridge)

@@ -1,0 +1,228 @@
+from contextlib import ExitStack
+
+import concourse.mybir as mybir
+
+I, J, L, R = 2048, 128, 32, 512
+FLOPS = 2 * I * J * L * R
+
+F32 = mybir.dt.float32
+BF16 = mybir.dt.bfloat16
+I32 = mybir.dt.int32
+U32 = mybir.dt.uint32
+U8 = mybir.dt.uint8
+E4M3X4 = mybir.dt.float8_e4m3fn_x4
+E5M2X4 = mybir.dt.float8_e5m2_x4
+MULT = mybir.AluOpType.mult
+ADD = mybir.AluOpType.add
+
+P = 128
+PASSES = J * L // 512
+TILES = I // P
+FIRST = 7
+FIRST_COLS = FIRST * P
+CHUNKS = ((7, 11), (11, 16))
+
+
+def tile_cp_factor_gradient_e1_kernel(tc, g_words, g_scales, b, c, a, weight, ridge, out):
+    nc = tc.nc
+    words = g_words.rearrange("g p n t -> g p (n t)").bitcast(I32)
+    scale_words = g_scales.bitcast(I32)
+
+    with ExitStack() as ctx:
+        keep = ctx.enter_context(tc.tile_pool(name="keep", bufs=1))
+        work = ctx.enter_context(tc.tile_pool(name="work", bufs=3))
+        psum = ctx.enter_context(tc.psum_pool(name="psum", bufs=1))
+        ctx.enter_context(tc.manual_schedule())
+
+        sc_first = keep.tile([P, PASSES, FIRST_COLS], U8, name="sc_first", align_bytes=64)
+        sc_rest = keep.tile([P, PASSES, I - FIRST_COLS], U8, name="sc_rest", align_bytes=64)
+        sc_first_w = sc_first[:].bitcast(I32)
+        sc_rest_w = sc_rest[:].bitcast(I32)
+
+        def load_scales(dst_w, g0, g1, w0, w1):
+            for q in range(4):
+                nc.sync.dma_start(
+                    out=dst_w[32 * q : 32 * q + 4, g0:g1, :],
+                    in_=scale_words[g0:g1, 4 * q : 4 * q + 4, w0:w1].rearrange("g q n -> q g n"),
+                )
+
+        b_rep = []
+        for g in range(PASSES):
+            b_rep.append(keep.tile([P, R], BF16, name="b_rep%d" % g))
+        c_rep = keep.tile([P, 4 * R], BF16, name="c_rep")
+
+        def load_b(g):
+            nc.sync.dma_start(out=b_rep[g][:], in_=b[16 * g : 16 * g + 16, :].unsqueeze(1).to_broadcast([16, 8, R]))
+
+        g_first = []
+        for g in range(PASSES):
+            g_first.append(keep.tile([P, FIRST_COLS], U32, name="g_first%d" % g, align_bytes=64))
+
+        def load_g(g):
+            nc.sync.dma_start(out=g_first[g][:].bitcast(I32), in_=words[g, :, 0:FIRST_COLS])
+
+        warm = keep.tile([P, 2], F32, name="warm")
+        nc.vector.memset(sc_first_w[:, 0:2, :], 0)
+        nc.gpsimd.memset(warm[:, 0:1], 0.0)
+        nc.scalar.copy(out=warm[:, 1:2], in_=warm[:, 0:1])
+        nc.gpsimd.memset(sc_rest_w, 0)
+        nc.vector.memset(sc_first_w[:, 2:8, :], 0)
+
+        load_b(0)
+        nc.sync.dma_start(
+            out=c_rep[:], in_=c.rearrange("(s t) r -> s (t r)", t=4).unsqueeze(0).to_broadcast([16, 8, 4 * R])
+        )
+        load_scales(sc_first_w, 0, 2, 0, FIRST_COLS // 4)
+        load_g(0)
+        load_b(1)
+        load_g(1)
+        load_scales(sc_first_w, 2, 8, 0, FIRST_COLS // 4)
+        for g in range(2, PASSES):
+            load_b(g)
+            load_g(g)
+        w_rep = keep.tile([P, R], BF16, name="w_rep")
+        r_rep = keep.tile([P, R], BF16, name="r_rep")
+        nc.sync.dma_start(out=r_rep[:], in_=ridge.partition_broadcast(P))
+        nc.sync.dma_start(out=w_rep[:], in_=weight.partition_broadcast(P))
+        a_tiles = a.rearrange("(n p) r -> p n r", p=P)
+        a_sb = []
+        for k in range(4):
+            a_sb.append(keep.tile([P, 4, R], BF16, name="a_sb%d" % k))
+
+        def load_a(k):
+            nc.sync.dma_start(out=a_sb[k][:], in_=a_tiles[:, 4 * k : 4 * k + 4, :])
+
+        g_rest = []
+        for k in range(len(CHUNKS)):
+            t0, t1 = CHUNKS[k]
+            g_rest.append(keep.tile([P, PASSES, (t1 - t0) * P], U32, name="g_rest%d" % k, align_bytes=64))
+
+        def load_rest(k):
+            t0, t1 = CHUNKS[k]
+            nc.sync.dma_start(
+                out=g_rest[k][:].bitcast(I32), in_=words[:, :, t0 * P : t1 * P].rearrange("g p n -> p g n")
+            )
+
+        load_a(0)
+        load_a(1)
+        load_scales(sc_rest_w, 0, 8, FIRST_COLS // 4, I // 4)
+        load_rest(0)
+        load_a(2)
+        load_rest(1)
+        load_a(3)
+
+        c_by_word = keep.tile([P, R, 4], BF16, name="c_by_word")
+        b_pairs = []
+        codes = []
+        code_scales = []
+        for g in range(PASSES):
+            b_pairs.append(keep.tile([P, R, 2], BF16, name="b_pairs%d" % g))
+            codes.append(keep.tile([P, R], U32, name="codes%d" % g, align_bytes=64))
+            code_scales.append(keep.tile([P, R], U8, name="code_scales%d" % g, align_bytes=64))
+
+        def pair_b(g):
+            nc.scalar.copy(out=b_pairs[g][:], in_=b_rep[g][:].unsqueeze(2).to_broadcast([P, R, 2]))
+
+        pair_b(0)
+        c_src = c_rep[:].rearrange("p (t r) -> p r t", t=4)
+        H = R // 2
+        V = 384
+        nc.vector.tensor_copy(out=c_by_word[:, 0:V, :], in_=c_src[:, 0:V, :])
+        nc.scalar.copy(out=c_by_word[:, V:R, :], in_=c_src[:, V:R, :])
+        for g in range(1, PASSES):
+            pair_b(g)
+
+        acc = []
+        for t in range(FIRST):
+            acc.append(psum.tile([P, R], F32, name="acc%d" % t, tag="bank%d" % t))
+
+        def multiply(t, g):
+            if t < FIRST:
+                w = g_first[g][:, t * P : (t + 1) * P]
+                s = sc_first[:, g, t * P : (t + 1) * P]
+            else:
+                k = 0 if t < CHUNKS[0][1] else 1
+                j = t - CHUNKS[k][0]
+                w = g_rest[k][:, g, j * P : (j + 1) * P]
+                s = sc_rest[:, g, (t - FIRST) * P : (t - FIRST + 1) * P]
+            nc.tensor.matmul_mx(
+                out=acc[t][:],
+                lhsT=w.bitcast(E5M2X4),
+                lhsT_scale=s,
+                rhs=codes[g][:].bitcast(E4M3X4),
+                rhs_scale=code_scales[g][:],
+                start=(g == 0),
+                stop=(g == PASSES - 1),
+            )
+
+        for g in range(PASSES):
+            kr = work.tile([P, R, 4], BF16, name="kr", align_bytes=64)
+            for h in range(2):
+                cols = slice(h * H, (h + 1) * H)
+                nc.vector.tensor_tensor(
+                    out=kr[:, cols, :].rearrange("p r (u e) -> p r u e", e=2),
+                    in0=c_by_word[:, cols, :].rearrange("p r (u e) -> p r u e", e=2),
+                    in1=b_pairs[g][:, cols, :].unsqueeze(2).to_broadcast([P, H, 2, 2]),
+                    op=MULT,
+                )
+            for h in range(2):
+                cols = slice(h * H, (h + 1) * H)
+                nc.vector.quantize_mx(
+                    out=codes[g][:, cols].bitcast(E4M3X4),
+                    scales=code_scales[g][:, cols],
+                    in_=kr[:, cols, :].rearrange("p r t -> p (r t)"),
+                )
+            for t in range(FIRST):
+                multiply(t, g)
+
+        ridge_part = keep.tile([P, TILES, R], F32, name="ridge_part")
+        result = keep.tile([P, TILES, R], F32, name="result")
+
+        def regularise(t):
+            nc.vector.tensor_tensor(out=ridge_part[:, t, :], in0=a_sb[t // 4][:, t % 4, :], in1=r_rep[:], op=MULT)
+
+        def weigh(t, c0=0, c1=R):
+            nc.vector.tensor_tensor(out=result[:, t, c0:c1], in0=acc[t][:, c0:c1], in1=w_rep[:, c0:c1], op=MULT)
+
+        def finish(engine, t, c0=0, c1=R):
+            engine.tensor_tensor(out=result[:, t, c0:c1], in0=result[:, t, c0:c1], in1=ridge_part[:, t, c0:c1], op=ADD)
+            nc.sync.dma_start(out=out[t * P : (t + 1) * P, c0:c1], in_=result[:, t, c0:c1])
+
+        def product(t):
+            acc.append(psum.tile([P, R], F32, name="acc%d" % t, tag="bank%d" % (t % 8)))
+            for g in range(PASSES):
+                multiply(t, g)
+
+        product(7)
+        for t in range(0, 4):
+            regularise(t)
+        for t in range(0, 7):
+            weigh(t)
+        for t in range(0, 3):
+            finish(nc.gpsimd, t)
+        for t in range(4, 7):
+            regularise(t)
+        for t in range(3, 7):
+            finish(nc.vector, t)
+        for t0 in (7, 10):
+            for t in range(t0 + 1, t0 + 4):
+                product(t)
+            for t in range(t0, t0 + 3):
+                regularise(t)
+            for t in range(t0, t0 + 3):
+                weigh(t)
+            finish(nc.gpsimd, t0)
+            finish(nc.vector, t0 + 1)
+            finish(nc.vector, t0 + 2)
+        product(14)
+        product(15)
+        for t in range(13, 16):
+            regularise(t)
+        weigh(13)
+        weigh(14)
+        finish(nc.vector, 13)
+        finish(nc.vector, 14)
+        weigh(15, 0, H)
+        weigh(15, H, R)
+        finish(nc.vector, 15, 0, H)
+        finish(nc.vector, 15, H, R)

@@ -1,6 +1,7 @@
 from contextlib import ExitStack
 
 import concourse.mybir as mybir
+from concourse.masks import make_identity
 
 I, J, L, R = 2048, 128, 32, 512
 FLOPS = 2 * I * J * L * R
@@ -20,7 +21,7 @@ PASSES = J * L // 512
 TILES = I // P
 FIRST = 7
 FIRST_COLS = FIRST * P
-CHUNKS = ((7, 11), (11, 16))
+CHUNKS = ((7, 9), (9, 12), (12, 16))
 
 
 def tile_cp_factor_gradient_e1_kernel(tc, g_words, g_scales, b, c, a, weight, ridge, out):
@@ -49,7 +50,9 @@ def tile_cp_factor_gradient_e1_kernel(tc, g_words, g_scales, b, c, a, weight, ri
         b_rep = []
         for g in range(PASSES):
             b_rep.append(keep.tile([P, R], BF16, name="b_rep%d" % g))
-        c_rep = keep.tile([P, 4 * R], BF16, name="c_rep")
+        small = keep.tile([P, R], BF16, name="small")
+        ident = keep.tile([P, P], BF16, name="ident")
+        ident_f32 = keep.tile([P, P], F32, name="ident_f32")
 
         def load_b(g):
             nc.sync.dma_start(out=b_rep[g][:], in_=b[16 * g : 16 * g + 16, :].unsqueeze(1).to_broadcast([16, 8, R]))
@@ -62,28 +65,30 @@ def tile_cp_factor_gradient_e1_kernel(tc, g_words, g_scales, b, c, a, weight, ri
             nc.sync.dma_start(out=g_first[g][:].bitcast(I32), in_=words[g, :, 0:FIRST_COLS])
 
         warm = keep.tile([P, 2], F32, name="warm")
-        nc.vector.memset(sc_first_w[:, 0:2, :], 0)
+        nc.vector.memset(small[L : 2 * L, :], 0.0)
+        nc.vector.memset(small[2 * L : P, :], 0.0)
         nc.gpsimd.memset(warm[:, 0:1], 0.0)
         nc.scalar.copy(out=warm[:, 1:2], in_=warm[:, 0:1])
+        nc.vector.memset(sc_first_w[:, 0:4, :], 0)
+        make_identity(nc, ident[:])
+        make_identity(nc, ident_f32[:])
+        nc.vector.memset(sc_first_w[:, 4:8, :], 0)
         nc.gpsimd.memset(sc_rest_w, 0)
-        nc.vector.memset(sc_first_w[:, 2:8, :], 0)
 
+        nc.sync.dma_start(out=small[0:L, :], in_=c)
         load_b(0)
-        nc.sync.dma_start(
-            out=c_rep[:], in_=c.rearrange("(s t) r -> s (t r)", t=4).unsqueeze(0).to_broadcast([16, 8, 4 * R])
-        )
-        load_scales(sc_first_w, 0, 2, 0, FIRST_COLS // 4)
+        nc.sync.dma_start(out=small[L : L + 1, :], in_=weight.unsqueeze(0))
+        nc.sync.dma_start(out=small[L + 1 : L + 2, :], in_=ridge.unsqueeze(0))
+        load_scales(sc_first_w, 0, 4, 0, FIRST_COLS // 4)
         load_g(0)
-        load_b(1)
-        load_g(1)
-        load_scales(sc_first_w, 2, 8, 0, FIRST_COLS // 4)
-        for g in range(2, PASSES):
+        for g in range(1, 4):
             load_b(g)
             load_g(g)
-        w_rep = keep.tile([P, R], BF16, name="w_rep")
-        r_rep = keep.tile([P, R], BF16, name="r_rep")
-        nc.sync.dma_start(out=r_rep[:], in_=ridge.partition_broadcast(P))
-        nc.sync.dma_start(out=w_rep[:], in_=weight.partition_broadcast(P))
+        load_scales(sc_first_w, 4, 8, 0, FIRST_COLS // 4)
+        load_scales(sc_rest_w, 0, 8, FIRST_COLS // 4, I // 4)
+        for g in range(4, PASSES):
+            load_b(g)
+            load_g(g)
         a_tiles = a.rearrange("(n p) r -> p n r", p=P)
         a_sb = []
         for k in range(4):
@@ -104,11 +109,11 @@ def tile_cp_factor_gradient_e1_kernel(tc, g_words, g_scales, b, c, a, weight, ri
             )
 
         load_a(0)
-        load_a(1)
-        load_scales(sc_rest_w, 0, 8, FIRST_COLS // 4, I // 4)
         load_rest(0)
-        load_a(2)
+        load_a(1)
         load_rest(1)
+        load_a(2)
+        load_rest(2)
         load_a(3)
 
         c_by_word = keep.tile([P, R, 4], BF16, name="c_by_word")
@@ -120,17 +125,62 @@ def tile_cp_factor_gradient_e1_kernel(tc, g_words, g_scales, b, c, a, weight, ri
             codes.append(keep.tile([P, R], U32, name="codes%d" % g, align_bytes=64))
             code_scales.append(keep.tile([P, R], U8, name="code_scales%d" % g, align_bytes=64))
 
-        def pair_b(g):
-            nc.scalar.copy(out=b_pairs[g][:], in_=b_rep[g][:].unsqueeze(2).to_broadcast([P, R, 2]))
+        def pair_b(copy, g):
+            copy(out=b_pairs[g][:], in_=b_rep[g][:].unsqueeze(2).to_broadcast([P, R, 2]))
 
-        pair_b(0)
-        c_src = c_rep[:].rearrange("p (t r) -> p r t", t=4)
         H = R // 2
-        V = 384
-        nc.vector.tensor_copy(out=c_by_word[:, 0:V, :], in_=c_src[:, 0:V, :])
-        nc.scalar.copy(out=c_by_word[:, V:R, :], in_=c_src[:, V:R, :])
-        for g in range(1, PASSES):
-            pair_b(g)
+        copies = (nc.vector.tensor_copy, nc.scalar.copy)
+        small_t = (
+            psum.tile([P, 2, P], BF16, name="small_t0", tag="bank7"),
+            psum.tile([P, 2, P], BF16, name="small_t1", tag="bank6"),
+        )
+        c_cols = keep.tile([P, 4, 2, P], F32, name="c_cols")
+        wr_cols = keep.tile([P, 2, 4], BF16, name="wr_cols")
+        for h in range(2):
+            for j in range(2):
+                m = 2 * h + j
+                nc.tensor.transpose(small_t[h][:, j, :], small[:, m * P : (m + 1) * P], ident[:])
+        for h in range(2):
+            pairs = small_t[h][:].bitcast(F32)[:, :, 0 : L // 2].rearrange("p m (s u) -> p u m s", u=2)
+            for u in range(2):
+                copies[h](
+                    out=c_cols[:, 2 * h : 2 * h + 2, u, :].rearrange("p m (q s) -> p m q s", s=8),
+                    in_=pairs[:, u, :, :].unsqueeze(2).to_broadcast([P, 2, 16, 8]),
+                )
+        for h in range(2):
+            nc.scalar.copy(
+                out=wr_cols[:, :, 2 * h : 2 * h + 2],
+                in_=small_t[h][:, :, L : L + 2].rearrange("p m x -> p x m"),
+            )
+        pair_b(nc.vector.tensor_copy, 0)
+        c_wide = (
+            psum.tile([P, 2, 2, P], F32, name="c_wide0", tag="bank5"),
+            psum.tile([P, 2, 2, P], F32, name="c_wide1", tag="bank4"),
+        )
+        for h in range(2):
+            for j in range(2):
+                for u in range(2):
+                    nc.tensor.transpose(c_wide[h][:, j, u, :], c_cols[:, 2 * h + j, u, :], ident_f32[:])
+        for h in range(2):
+            copies[h](
+                out=c_by_word[:, h * H : (h + 1) * H, :]
+                .rearrange("p r t -> p (r t)")
+                .bitcast(F32)
+                .rearrange("p (m r u) -> p m r u", m=2, u=2),
+                in_=c_wide[h][:].rearrange("p m u r -> p m r u"),
+            )
+        wr_wide = psum.tile([P, 2, R], BF16, name="wr_wide", tag="bank7")
+        for x in range(2):
+            for m in range(4):
+                nc.tensor.transpose(
+                    wr_wide[:, x, m * P : (m + 1) * P], wr_cols[:, x, m : m + 1].to_broadcast([P, P]), ident[:]
+                )
+        wr_rep = keep.tile([P, 2, R], BF16, name="wr_rep")
+        pair_b(nc.scalar.copy, 1)
+        pair_b(nc.scalar.copy, 2)
+        nc.scalar.copy(out=wr_rep[:], in_=wr_wide[:])
+        for g in range(3, PASSES):
+            pair_b(nc.scalar.copy, g)
 
         acc = []
         for t in range(FIRST):
@@ -141,7 +191,9 @@ def tile_cp_factor_gradient_e1_kernel(tc, g_words, g_scales, b, c, a, weight, ri
                 w = g_first[g][:, t * P : (t + 1) * P]
                 s = sc_first[:, g, t * P : (t + 1) * P]
             else:
-                k = 0 if t < CHUNKS[0][1] else 1
+                k = 0
+                while t >= CHUNKS[k][1]:
+                    k = k + 1
                 j = t - CHUNKS[k][0]
                 w = g_rest[k][:, g, j * P : (j + 1) * P]
                 s = sc_rest[:, g, (t - FIRST) * P : (t - FIRST + 1) * P]
@@ -179,10 +231,10 @@ def tile_cp_factor_gradient_e1_kernel(tc, g_words, g_scales, b, c, a, weight, ri
         result = keep.tile([P, TILES, R], F32, name="result")
 
         def regularise(t):
-            nc.vector.tensor_tensor(out=ridge_part[:, t, :], in0=a_sb[t // 4][:, t % 4, :], in1=r_rep[:], op=MULT)
+            nc.vector.tensor_tensor(out=ridge_part[:, t, :], in0=a_sb[t // 4][:, t % 4, :], in1=wr_rep[:, 1, :], op=MULT)
 
         def weigh(t, c0=0, c1=R):
-            nc.vector.tensor_tensor(out=result[:, t, c0:c1], in0=acc[t][:, c0:c1], in1=w_rep[:, c0:c1], op=MULT)
+            nc.vector.tensor_tensor(out=result[:, t, c0:c1], in0=acc[t][:, c0:c1], in1=wr_rep[:, 0, c0:c1], op=MULT)
 
         def finish(engine, t, c0=0, c1=R):
             engine.tensor_tensor(out=result[:, t, c0:c1], in0=result[:, t, c0:c1], in1=ridge_part[:, t, c0:c1], op=ADD)

@@ -22,12 +22,13 @@ TILES = I // P
 FIRST = 7
 FIRST_COLS = FIRST * P
 CHUNKS = ((7, 9), (9, 12), (12, 16))
+H = R // 2
 
 
 def tile_cp_factor_gradient_e1_kernel(tc, g_words, g_scales, b, c, a, weight, ridge, out):
     nc = tc.nc
     words = g_words.rearrange("g p n t -> g p (n t)").bitcast(I32)
-    scale_words = g_scales.bitcast(I32)
+    scale_words = g_scales.bitcast(I32).rearrange("g q n -> q g n")
 
     with ExitStack() as ctx:
         keep = ctx.enter_context(tc.tile_pool(name="keep", bufs=1))
@@ -35,72 +36,30 @@ def tile_cp_factor_gradient_e1_kernel(tc, g_words, g_scales, b, c, a, weight, ri
         psum = ctx.enter_context(tc.psum_pool(name="psum", bufs=1))
         ctx.enter_context(tc.manual_schedule())
 
-        sc_first = keep.tile([P, PASSES, FIRST_COLS], U8, name="sc_first", align_bytes=64)
-        sc_rest = keep.tile([P, PASSES, I - FIRST_COLS], U8, name="sc_rest", align_bytes=64)
-        sc_first_w = sc_first[:].bitcast(I32)
-        sc_rest_w = sc_rest[:].bitcast(I32)
-
-        def load_scales(dst_w, g0, g1, w0, w1):
-            for q in range(4):
-                nc.sync.dma_start(
-                    out=dst_w[32 * q : 32 * q + 4, g0:g1, :],
-                    in_=scale_words[g0:g1, 4 * q : 4 * q + 4, w0:w1].rearrange("g q n -> q g n"),
-                )
-
-        b_rep = []
-        for g in range(PASSES):
-            b_rep.append(keep.tile([P, R], BF16, name="b_rep%d" % g))
+        scales = keep.tile([P, PASSES, I], U8, name="scales", align_bytes=64)
+        scales_w = scales[:].bitcast(I32)
         small = keep.tile([P, R], BF16, name="small")
         ident = keep.tile([P, P], BF16, name="ident")
         ident_f32 = keep.tile([P, P], F32, name="ident_f32")
-
-        def load_b(g):
-            nc.sync.dma_start(out=b_rep[g][:], in_=b[16 * g : 16 * g + 16, :].unsqueeze(1).to_broadcast([16, 8, R]))
-
-        g_first = []
-        for g in range(PASSES):
-            g_first.append(keep.tile([P, FIRST_COLS], U32, name="g_first%d" % g, align_bytes=64))
-
-        def load_g(g):
-            nc.sync.dma_start(out=g_first[g][:].bitcast(I32), in_=words[g, :, 0:FIRST_COLS])
-
         warm = keep.tile([P, 2], F32, name="warm")
-        nc.vector.memset(small[L : 2 * L, :], 0.0)
-        nc.vector.memset(small[2 * L : P, :], 0.0)
-        nc.gpsimd.memset(warm[:, 0:1], 0.0)
-        nc.scalar.copy(out=warm[:, 1:2], in_=warm[:, 0:1])
-        nc.vector.memset(sc_first_w[:, 0:4, :], 0)
-        make_identity(nc, ident[:])
-        make_identity(nc, ident_f32[:])
-        nc.vector.memset(sc_first_w[:, 4:8, :], 0)
-        nc.gpsimd.memset(sc_rest_w, 0)
-
-        nc.sync.dma_start(out=small[0:L, :], in_=c)
-        load_b(0)
-        nc.sync.dma_start(out=small[L : L + 1, :], in_=weight.unsqueeze(0))
-        nc.sync.dma_start(out=small[L + 1 : L + 2, :], in_=ridge.unsqueeze(0))
-        load_scales(sc_first_w, 0, 4, 0, FIRST_COLS // 4)
-        load_g(0)
-        for g in range(1, 4):
-            load_b(g)
-            load_g(g)
-        load_scales(sc_first_w, 4, 8, 0, FIRST_COLS // 4)
-        load_scales(sc_rest_w, 0, 8, FIRST_COLS // 4, I // 4)
-        for g in range(4, PASSES):
-            load_b(g)
-            load_g(g)
-        a_tiles = a.rearrange("(n p) r -> p n r", p=P)
         a_sb = []
         for k in range(4):
             a_sb.append(keep.tile([P, 4, R], BF16, name="a_sb%d" % k))
-
-        def load_a(k):
-            nc.sync.dma_start(out=a_sb[k][:], in_=a_tiles[:, 4 * k : 4 * k + 4, :])
-
+        b_rep = []
+        g_first = []
+        for g in range(PASSES):
+            b_rep.append(keep.tile([P, R], BF16, name="b_rep%d" % g))
+            g_first.append(keep.tile([P, FIRST_COLS], U32, name="g_first%d" % g, align_bytes=64))
         g_rest = []
         for k in range(len(CHUNKS)):
             t0, t1 = CHUNKS[k]
             g_rest.append(keep.tile([P, PASSES, (t1 - t0) * P], U32, name="g_rest%d" % k, align_bytes=64))
+
+        def load_b(g):
+            nc.sync.dma_start(out=b_rep[g][:], in_=b[16 * g : 16 * g + 16, :].unsqueeze(1).to_broadcast([16, 8, R]))
+
+        def load_g(g):
+            nc.sync.dma_start(out=g_first[g][:].bitcast(I32), in_=words[g, :, 0:FIRST_COLS])
 
         def load_rest(k):
             t0, t1 = CHUNKS[k]
@@ -108,12 +67,49 @@ def tile_cp_factor_gradient_e1_kernel(tc, g_words, g_scales, b, c, a, weight, ri
                 out=g_rest[k][:].bitcast(I32), in_=words[:, :, t0 * P : t1 * P].rearrange("g p n -> p g n")
             )
 
-        load_a(0)
+        def load_scales(g0, g1, c0, c1):
+            for r in range(4):
+                nc.sync.dma_start(
+                    out=scales_w[r:P:32, g0:g1, c0 // 4 : c1 // 4],
+                    in_=scale_words[r:16:4, g0:g1, c0 // 4 : c1 // 4],
+                )
+
+        a_tiles = a.rearrange("(n p) r -> p n r", p=P)
+        out_tiles = out.rearrange("(n p) r -> p n r", p=P)
+
+        def load_a(k):
+            nc.sync.dma_start(out=a_sb[k][:], in_=a_tiles[:, 4 * k : 4 * k + 4, :])
+
+        nc.gpsimd.memset(warm[:, 0:1], 0.0)
+        nc.scalar.copy(out=warm[:, 1:2], in_=warm[:, 0:1])
+        nc.vector.memset(small[L : 2 * L, :], 0.0)
+        nc.vector.memset(small[2 * L : P, :], 0.0)
+        nc.vector.memset(scales_w[:, 0:2, 0 : FIRST_COLS // 4], 0)
+        nc.vector.memset(scales_w[:, 2:8, 0 : FIRST_COLS // 4], 0)
+        make_identity(nc, ident[:])
+        make_identity(nc, ident_f32[:])
+        nc.gpsimd.memset(scales_w[:, :, FIRST_COLS // 4 : I // 4], 0)
+
+        nc.sync.dma_start(out=small[0:L, :], in_=c)
+        load_b(0)
+        nc.sync.dma_start(out=small[L : L + 1, :], in_=weight.unsqueeze(0))
+        nc.sync.dma_start(out=small[L + 1 : L + 2, :], in_=ridge.unsqueeze(0))
+        load_scales(0, 2, 0, FIRST_COLS)
+        load_g(0)
+        for g in (1, 2):
+            load_b(g)
+            load_g(g)
+        load_scales(2, 8, 0, FIRST_COLS)
+        for g in range(3, PASSES):
+            load_b(g)
+            load_g(g)
         load_rest(0)
+        load_scales(0, 8, FIRST_COLS, I)
+        load_a(0)
         load_a(1)
         load_rest(1)
-        load_a(2)
         load_rest(2)
+        load_a(2)
         load_a(3)
 
         c_by_word = keep.tile([P, R, 4], BF16, name="c_by_word")
@@ -128,46 +124,45 @@ def tile_cp_factor_gradient_e1_kernel(tc, g_words, g_scales, b, c, a, weight, ri
         def pair_b(copy, g):
             copy(out=b_pairs[g][:], in_=b_rep[g][:].unsqueeze(2).to_broadcast([P, R, 2]))
 
-        H = R // 2
         copies = (nc.vector.tensor_copy, nc.scalar.copy)
         small_t = (
-            psum.tile([P, 2, P], BF16, name="small_t0", tag="bank7"),
+            psum.tile([P, 2, P], BF16, name="small_t0", tag="bank3"),
             psum.tile([P, 2, P], BF16, name="small_t1", tag="bank6"),
         )
         c_cols = keep.tile([P, 4, 2, P], F32, name="c_cols")
         wr_cols = keep.tile([P, 2, 4], BF16, name="wr_cols")
-        for h in range(2):
+        for d in range(2):
             for j in range(2):
-                m = 2 * h + j
-                nc.tensor.transpose(small_t[h][:, j, :], small[:, m * P : (m + 1) * P], ident[:])
-        for h in range(2):
-            pairs = small_t[h][:].bitcast(F32)[:, :, 0 : L // 2].rearrange("p m (s u) -> p u m s", u=2)
+                m = 2 * d + j
+                nc.tensor.transpose(small_t[d][:, j, :], small[:, m * P : (m + 1) * P], ident[:])
+        for d in range(2):
+            pairs = small_t[d][:].bitcast(F32)[:, :, 0 : L // 2].rearrange("p m (s u) -> p u m s", u=2)
             for u in range(2):
-                copies[h](
-                    out=c_cols[:, 2 * h : 2 * h + 2, u, :].rearrange("p m (q s) -> p m q s", s=8),
+                copies[d](
+                    out=c_cols[:, 2 * d : 2 * d + 2, u, :].rearrange("p m (q s) -> p m q s", s=8),
                     in_=pairs[:, u, :, :].unsqueeze(2).to_broadcast([P, 2, 16, 8]),
                 )
-        for h in range(2):
+        for d in range(2):
             nc.scalar.copy(
-                out=wr_cols[:, :, 2 * h : 2 * h + 2],
-                in_=small_t[h][:, :, L : L + 2].rearrange("p m x -> p x m"),
+                out=wr_cols[:, :, 2 * d : 2 * d + 2],
+                in_=small_t[d][:, :, L : L + 2].rearrange("p m x -> p x m"),
             )
         pair_b(nc.vector.tensor_copy, 0)
         c_wide = (
             psum.tile([P, 2, 2, P], F32, name="c_wide0", tag="bank5"),
             psum.tile([P, 2, 2, P], F32, name="c_wide1", tag="bank4"),
         )
-        for h in range(2):
+        for d in range(2):
             for j in range(2):
                 for u in range(2):
-                    nc.tensor.transpose(c_wide[h][:, j, u, :], c_cols[:, 2 * h + j, u, :], ident_f32[:])
-        for h in range(2):
-            copies[h](
-                out=c_by_word[:, h * H : (h + 1) * H, :]
+                    nc.tensor.transpose(c_wide[d][:, j, u, :], c_cols[:, 2 * d + j, u, :], ident_f32[:])
+        for d in range(2):
+            copies[d](
+                out=c_by_word[:, d * H : (d + 1) * H, :]
                 .rearrange("p r t -> p (r t)")
                 .bitcast(F32)
                 .rearrange("p (m r u) -> p m r u", m=2, u=2),
-                in_=c_wide[h][:].rearrange("p m u r -> p m r u"),
+                in_=c_wide[d][:].rearrange("p m u r -> p m r u"),
             )
         wr_wide = psum.tile([P, 2, R], BF16, name="wr_wide", tag="bank7")
         for x in range(2):
@@ -175,10 +170,10 @@ def tile_cp_factor_gradient_e1_kernel(tc, g_words, g_scales, b, c, a, weight, ri
                 nc.tensor.transpose(
                     wr_wide[:, x, m * P : (m + 1) * P], wr_cols[:, x, m : m + 1].to_broadcast([P, P]), ident[:]
                 )
-        wr_rep = keep.tile([P, 2, R], BF16, name="wr_rep")
+        w_rep = keep.tile([P, R], BF16, name="w_rep")
         pair_b(nc.scalar.copy, 1)
         pair_b(nc.scalar.copy, 2)
-        nc.scalar.copy(out=wr_rep[:], in_=wr_wide[:])
+        nc.scalar.copy(out=w_rep[:], in_=wr_wide[:, 0, :])
         for g in range(3, PASSES):
             pair_b(nc.scalar.copy, g)
 
@@ -189,18 +184,16 @@ def tile_cp_factor_gradient_e1_kernel(tc, g_words, g_scales, b, c, a, weight, ri
         def multiply(t, g):
             if t < FIRST:
                 w = g_first[g][:, t * P : (t + 1) * P]
-                s = sc_first[:, g, t * P : (t + 1) * P]
             else:
                 k = 0
                 while t >= CHUNKS[k][1]:
                     k = k + 1
                 j = t - CHUNKS[k][0]
                 w = g_rest[k][:, g, j * P : (j + 1) * P]
-                s = sc_rest[:, g, (t - FIRST) * P : (t - FIRST + 1) * P]
             nc.tensor.matmul_mx(
                 out=acc[t][:],
                 lhsT=w.bitcast(E5M2X4),
-                lhsT_scale=s,
+                lhsT_scale=scales[:, g, t * P : (t + 1) * P],
                 rhs=codes[g][:].bitcast(E4M3X4),
                 rhs_scale=code_scales[g][:],
                 start=(g == 0),
@@ -209,16 +202,16 @@ def tile_cp_factor_gradient_e1_kernel(tc, g_words, g_scales, b, c, a, weight, ri
 
         for g in range(PASSES):
             kr = work.tile([P, R, 4], BF16, name="kr", align_bytes=64)
-            for h in range(2):
-                cols = slice(h * H, (h + 1) * H)
+            for d in range(2):
+                cols = slice(d * H, (d + 1) * H)
                 nc.vector.tensor_tensor(
                     out=kr[:, cols, :].rearrange("p r (u e) -> p r u e", e=2),
                     in0=c_by_word[:, cols, :].rearrange("p r (u e) -> p r u e", e=2),
                     in1=b_pairs[g][:, cols, :].unsqueeze(2).to_broadcast([P, H, 2, 2]),
                     op=MULT,
                 )
-            for h in range(2):
-                cols = slice(h * H, (h + 1) * H)
+            for d in range(2):
+                cols = slice(d * H, (d + 1) * H)
                 nc.vector.quantize_mx(
                     out=codes[g][:, cols].bitcast(E4M3X4),
                     scales=code_scales[g][:, cols],
@@ -231,50 +224,39 @@ def tile_cp_factor_gradient_e1_kernel(tc, g_words, g_scales, b, c, a, weight, ri
         result = keep.tile([P, TILES, R], F32, name="result")
 
         def regularise(t):
-            nc.vector.tensor_tensor(out=ridge_part[:, t, :], in0=a_sb[t // 4][:, t % 4, :], in1=wr_rep[:, 1, :], op=MULT)
+            for n in (t, t + 1):
+                nc.vector.tensor_tensor(
+                    out=ridge_part[:, n, :], in0=a_sb[n // 4][:, n % 4, :], in1=wr_wide[:, 1, :], op=MULT
+                )
 
         def weigh(t, c0=0, c1=R):
-            nc.vector.tensor_tensor(out=result[:, t, c0:c1], in0=acc[t][:, c0:c1], in1=wr_rep[:, 0, c0:c1], op=MULT)
+            nc.vector.tensor_tensor(out=result[:, t, c0:c1], in0=acc[t][:, c0:c1], in1=w_rep[:, c0:c1], op=MULT)
 
         def finish(engine, t, c0=0, c1=R):
-            engine.tensor_tensor(out=result[:, t, c0:c1], in0=result[:, t, c0:c1], in1=ridge_part[:, t, c0:c1], op=ADD)
-            nc.sync.dma_start(out=out[t * P : (t + 1) * P, c0:c1], in_=result[:, t, c0:c1])
+            part = result[:, t, c0:c1]
+            engine.tensor_tensor(out=part, in0=part, in1=ridge_part[:, t, c0:c1], op=ADD)
+            nc.sync.dma_start(out=out_tiles[:, t, c0:c1], in_=part)
 
         def product(t):
-            acc.append(psum.tile([P, R], F32, name="acc%d" % t, tag="bank%d" % (t % 8)))
+            acc.append(psum.tile([P, R], F32, name="acc%d" % t, tag="bank%d" % (t % 7)))
             for g in range(PASSES):
                 multiply(t, g)
 
-        product(7)
-        for t in range(0, 4):
-            regularise(t)
-        for t in range(0, 7):
+        ridge_after = {3: 0, 5: 2, 6: 4, 7: 6, 8: 8, 10: 10, 11: 12, 12: 14}
+        finished = 0
+        regular = 0
+        for t in range(TILES - 1):
             weigh(t)
-        for t in range(0, 3):
-            finish(nc.gpsimd, t)
-        for t in range(4, 7):
-            regularise(t)
-        for t in range(3, 7):
-            finish(nc.vector, t)
-        for t0 in (7, 10):
-            for t in range(t0 + 1, t0 + 4):
-                product(t)
-            for t in range(t0, t0 + 3):
-                regularise(t)
-            for t in range(t0, t0 + 3):
-                weigh(t)
-            finish(nc.gpsimd, t0)
-            finish(nc.vector, t0 + 1)
-            finish(nc.vector, t0 + 2)
-        product(14)
-        product(15)
-        for t in range(13, 16):
-            regularise(t)
-        weigh(13)
-        weigh(14)
-        finish(nc.vector, 13)
-        finish(nc.vector, 14)
-        weigh(15, 0, H)
-        weigh(15, H, R)
-        finish(nc.vector, 15, 0, H)
-        finish(nc.vector, 15, H, R)
+            if t + 7 < TILES:
+                product(t + 7)
+            if t in ridge_after:
+                regularise(ridge_after[t])
+                regular = ridge_after[t] + 2
+            while finished < min(regular, t + 1):
+                finish(nc.gpsimd, finished)
+                finished = finished + 1
+        last = TILES - 1
+        weigh(last, 0, H)
+        weigh(last, H, R)
+        finish(nc.vector, last, 0, H)
+        finish(nc.vector, last, H, R)

@@ -21,7 +21,7 @@ PASSES = J * L // 512
 TILES = I // P
 FIRST = 7
 FIRST_COLS = FIRST * P
-CHUNKS = ((7, 9), (9, 12), (12, 16))
+CHUNKS = ((7, 9), (9, 12), (12, 14), (14, 16))
 H = R // 2
 
 
@@ -94,8 +94,8 @@ def tile_cp_factor_gradient_e1_kernel(tc, g_words, g_scales, b, c, a, weight, ri
         load_b(0)
         nc.sync.dma_start(out=small[L : L + 1, :], in_=weight.unsqueeze(0))
         nc.sync.dma_start(out=small[L + 1 : L + 2, :], in_=ridge.unsqueeze(0))
-        load_scales(0, 2, 0, FIRST_COLS)
         load_g(0)
+        load_scales(0, 2, 0, FIRST_COLS)
         for g in (1, 2):
             load_b(g)
             load_g(g)
@@ -104,25 +104,30 @@ def tile_cp_factor_gradient_e1_kernel(tc, g_words, g_scales, b, c, a, weight, ri
             load_b(g)
             load_g(g)
         load_rest(0)
-        load_scales(0, 8, FIRST_COLS, I)
+        load_scales(0, 8, FIRST_COLS, 9 * P)
         load_a(0)
-        load_a(1)
         load_rest(1)
+        load_scales(0, 8, 9 * P, I)
+        load_a(1)
         load_rest(2)
         load_a(2)
         load_a(3)
+        load_rest(3)
 
         c_by_word = keep.tile([P, R, 4], BF16, name="c_by_word")
+        b_fours = []
         b_pairs = []
         codes = []
         code_scales = []
         for g in range(PASSES):
-            b_pairs.append(keep.tile([P, R, 2], BF16, name="b_pairs%d" % g))
+            b_fours.append(keep.tile([P, H, 4], BF16, name="b_fours%d" % g))
+            b_pairs.append(keep.tile([P, H, 2], BF16, name="b_pairs%d" % g))
             codes.append(keep.tile([P, R], U32, name="codes%d" % g, align_bytes=64))
             code_scales.append(keep.tile([P, R], U8, name="code_scales%d" % g, align_bytes=64))
 
         def pair_b(copy, g):
-            copy(out=b_pairs[g][:], in_=b_rep[g][:].unsqueeze(2).to_broadcast([P, R, 2]))
+            copy(out=b_fours[g][:], in_=b_rep[g][:, 0:H].unsqueeze(2).to_broadcast([P, H, 4]))
+            copy(out=b_pairs[g][:], in_=b_rep[g][:, H:R].unsqueeze(2).to_broadcast([P, H, 2]))
 
         copies = (nc.vector.tensor_copy, nc.scalar.copy)
         small_t = (
@@ -202,14 +207,13 @@ def tile_cp_factor_gradient_e1_kernel(tc, g_words, g_scales, b, c, a, weight, ri
 
         for g in range(PASSES):
             kr = work.tile([P, R, 4], BF16, name="kr", align_bytes=64)
-            for d in range(2):
-                cols = slice(d * H, (d + 1) * H)
-                nc.vector.tensor_tensor(
-                    out=kr[:, cols, :].rearrange("p r (u e) -> p r u e", e=2),
-                    in0=c_by_word[:, cols, :].rearrange("p r (u e) -> p r u e", e=2),
-                    in1=b_pairs[g][:, cols, :].unsqueeze(2).to_broadcast([P, H, 2, 2]),
-                    op=MULT,
-                )
+            nc.vector.tensor_tensor(out=kr[:, 0:H, :], in0=c_by_word[:, 0:H, :], in1=b_fours[g][:], op=MULT)
+            nc.vector.tensor_tensor(
+                out=kr[:, H:R, :].rearrange("p r (u e) -> p r u e", e=2),
+                in0=c_by_word[:, H:R, :].rearrange("p r (u e) -> p r u e", e=2),
+                in1=b_pairs[g][:].unsqueeze(2).to_broadcast([P, H, 2, 2]),
+                op=MULT,
+            )
             for d in range(2):
                 cols = slice(d * H, (d + 1) * H)
                 nc.vector.quantize_mx(
@@ -242,19 +246,24 @@ def tile_cp_factor_gradient_e1_kernel(tc, g_words, g_scales, b, c, a, weight, ri
             for g in range(PASSES):
                 multiply(t, g)
 
-        ridge_after = {3: 0, 5: 2, 6: 4, 7: 6, 8: 8, 10: 10, 11: 12, 12: 14}
-        finished = 0
+        ridge_after = {1: 0, 3: 2, 5: 4, 6: 6, 7: 8, 9: 10, 10: 12, 11: 14}
         regular = 0
-        for t in range(TILES - 1):
+        finished = 0
+        for t in range(14):
             weigh(t)
             if t + 7 < TILES:
                 product(t + 7)
             if t in ridge_after:
                 regularise(ridge_after[t])
                 regular = ridge_after[t] + 2
-            while finished < min(regular, t + 1):
+            while finished < min(regular, t + 1, 11):
                 finish(nc.gpsimd, finished)
                 finished = finished + 1
+        finish(nc.vector, 11)
+        finish(nc.vector, 12)
+        weigh(14)
+        finish(nc.vector, 13)
+        finish(nc.vector, 14)
         last = TILES - 1
         weigh(last, 0, H)
         weigh(last, H, R)

from contextlib import ExitStack

import concourse.mybir as mybir
from concourse.masks import make_identity

I, J, L, R = 2048, 128, 32, 512
FLOPS = 2 * I * J * L * R

F32 = mybir.dt.float32
BF16 = mybir.dt.bfloat16
I32 = mybir.dt.int32
U32 = mybir.dt.uint32
U8 = mybir.dt.uint8
E4M3X4 = mybir.dt.float8_e4m3fn_x4
E5M2X4 = mybir.dt.float8_e5m2_x4
MULT = mybir.AluOpType.mult
ADD = mybir.AluOpType.add

P = 128
PASSES = J * L // 512
TILES = I // P
FIRST = 7
FIRST_COLS = FIRST * P
CHUNKS = ((7, 9), (9, 12), (12, 14), (14, 16))
H = R // 2


def tile_cp_factor_gradient_e1_kernel(tc, g_words, g_scales, b, c, a, weight, ridge, out):
    nc = tc.nc
    words = g_words.rearrange("g p n t -> g p (n t)").bitcast(I32)
    scale_words = g_scales.bitcast(I32).rearrange("g q n -> q g n")

    with ExitStack() as ctx:
        keep = ctx.enter_context(tc.tile_pool(name="keep", bufs=1))
        work = ctx.enter_context(tc.tile_pool(name="work", bufs=3))
        psum = ctx.enter_context(tc.psum_pool(name="psum", bufs=1))
        ctx.enter_context(tc.manual_schedule())

        scales = keep.tile([P, PASSES, I], U8, name="scales", align_bytes=64)
        scales_w = scales[:].bitcast(I32)
        small = keep.tile([P, R], BF16, name="small")
        ident = keep.tile([P, P], BF16, name="ident")
        ident_f32 = keep.tile([P, P], F32, name="ident_f32")
        warm = keep.tile([P, 2], F32, name="warm")
        a_sb = []
        for k in range(4):
            a_sb.append(keep.tile([P, 4, R], BF16, name="a_sb%d" % k))
        b_rep = []
        g_first = []
        for g in range(PASSES):
            b_rep.append(keep.tile([P, R], BF16, name="b_rep%d" % g))
            g_first.append(keep.tile([P, FIRST_COLS], U32, name="g_first%d" % g, align_bytes=64))
        g_rest = []
        for k in range(len(CHUNKS)):
            t0, t1 = CHUNKS[k]
            g_rest.append(keep.tile([P, PASSES, (t1 - t0) * P], U32, name="g_rest%d" % k, align_bytes=64))

        def load_b(g):
            nc.sync.dma_start(out=b_rep[g][:], in_=b[16 * g : 16 * g + 16, :].unsqueeze(1).to_broadcast([16, 8, R]))

        def load_g(g):
            nc.sync.dma_start(out=g_first[g][:].bitcast(I32), in_=words[g, :, 0:FIRST_COLS])

        def load_rest(k):
            t0, t1 = CHUNKS[k]
            nc.sync.dma_start(
                out=g_rest[k][:].bitcast(I32), in_=words[:, :, t0 * P : t1 * P].rearrange("g p n -> p g n")
            )

        def load_scales(g0, g1, c0, c1):
            for r in range(4):
                nc.sync.dma_start(
                    out=scales_w[r:P:32, g0:g1, c0 // 4 : c1 // 4],
                    in_=scale_words[r:16:4, g0:g1, c0 // 4 : c1 // 4],
                )

        a_tiles = a.rearrange("(n p) r -> p n r", p=P)
        out_tiles = out.rearrange("(n p) r -> p n r", p=P)

        def load_a(k):
            nc.sync.dma_start(out=a_sb[k][:], in_=a_tiles[:, 4 * k : 4 * k + 4, :])

        nc.gpsimd.memset(warm[:, 0:1], 0.0)
        nc.scalar.copy(out=warm[:, 1:2], in_=warm[:, 0:1])
        nc.vector.memset(small[L : 2 * L, :], 0.0)
        nc.vector.memset(small[2 * L : P, :], 0.0)
        nc.vector.memset(scales_w[:, 0:2, 0 : FIRST_COLS // 4], 0)
        nc.vector.memset(scales_w[:, 2:8, 0 : FIRST_COLS // 4], 0)
        make_identity(nc, ident[:])
        make_identity(nc, ident_f32[:])
        nc.gpsimd.memset(scales_w[:, :, FIRST_COLS // 4 : I // 4], 0)

        nc.sync.dma_start(out=small[0:L, :], in_=c)
        load_b(0)
        nc.sync.dma_start(out=small[L : L + 1, :], in_=weight.unsqueeze(0))
        nc.sync.dma_start(out=small[L + 1 : L + 2, :], in_=ridge.unsqueeze(0))
        load_g(0)
        load_scales(0, 2, 0, FIRST_COLS)
        for g in (1, 2):
            load_b(g)
            load_g(g)
        load_scales(2, 8, 0, FIRST_COLS)
        for g in range(3, PASSES):
            load_b(g)
            load_g(g)
        load_rest(0)
        load_scales(0, 8, FIRST_COLS, 9 * P)
        load_a(0)
        load_rest(1)
        load_scales(0, 8, 9 * P, I)
        load_a(1)
        load_rest(2)
        load_a(2)
        load_a(3)
        load_rest(3)

        c_by_word = keep.tile([P, R, 4], BF16, name="c_by_word")
        b_fours = []
        b_pairs = []
        codes = []
        code_scales = []
        for g in range(PASSES):
            b_fours.append(keep.tile([P, H, 4], BF16, name="b_fours%d" % g))
            b_pairs.append(keep.tile([P, H, 2], BF16, name="b_pairs%d" % g))
            codes.append(keep.tile([P, R], U32, name="codes%d" % g, align_bytes=64))
            code_scales.append(keep.tile([P, R], U8, name="code_scales%d" % g, align_bytes=64))

        def pair_b(copy, g):
            copy(out=b_fours[g][:], in_=b_rep[g][:, 0:H].unsqueeze(2).to_broadcast([P, H, 4]))
            copy(out=b_pairs[g][:], in_=b_rep[g][:, H:R].unsqueeze(2).to_broadcast([P, H, 2]))

        copies = (nc.vector.tensor_copy, nc.scalar.copy)
        small_t = (
            psum.tile([P, 2, P], BF16, name="small_t0", tag="bank3"),
            psum.tile([P, 2, P], BF16, name="small_t1", tag="bank6"),
        )
        c_cols = keep.tile([P, 4, 2, P], F32, name="c_cols")
        wr_cols = keep.tile([P, 2, 4], BF16, name="wr_cols")
        for d in range(2):
            for j in range(2):
                m = 2 * d + j
                nc.tensor.transpose(small_t[d][:, j, :], small[:, m * P : (m + 1) * P], ident[:])
        for d in range(2):
            pairs = small_t[d][:].bitcast(F32)[:, :, 0 : L // 2].rearrange("p m (s u) -> p u m s", u=2)
            for u in range(2):
                copies[d](
                    out=c_cols[:, 2 * d : 2 * d + 2, u, :].rearrange("p m (q s) -> p m q s", s=8),
                    in_=pairs[:, u, :, :].unsqueeze(2).to_broadcast([P, 2, 16, 8]),
                )
        for d in range(2):
            nc.scalar.copy(
                out=wr_cols[:, :, 2 * d : 2 * d + 2],
                in_=small_t[d][:, :, L : L + 2].rearrange("p m x -> p x m"),
            )
        pair_b(nc.vector.tensor_copy, 0)
        c_wide = (
            psum.tile([P, 2, 2, P], F32, name="c_wide0", tag="bank5"),
            psum.tile([P, 2, 2, P], F32, name="c_wide1", tag="bank4"),
        )
        for d in range(2):
            for j in range(2):
                for u in range(2):
                    nc.tensor.transpose(c_wide[d][:, j, u, :], c_cols[:, 2 * d + j, u, :], ident_f32[:])
        for d in range(2):
            copies[d](
                out=c_by_word[:, d * H : (d + 1) * H, :]
                .rearrange("p r t -> p (r t)")
                .bitcast(F32)
                .rearrange("p (m r u) -> p m r u", m=2, u=2),
                in_=c_wide[d][:].rearrange("p m u r -> p m r u"),
            )
        wr_wide = psum.tile([P, 2, R], BF16, name="wr_wide", tag="bank7")
        for x in range(2):
            for m in range(4):
                nc.tensor.transpose(
                    wr_wide[:, x, m * P : (m + 1) * P], wr_cols[:, x, m : m + 1].to_broadcast([P, P]), ident[:]
                )
        w_rep = keep.tile([P, R], BF16, name="w_rep")
        pair_b(nc.scalar.copy, 1)
        pair_b(nc.scalar.copy, 2)
        nc.scalar.copy(out=w_rep[:], in_=wr_wide[:, 0, :])
        for g in range(3, PASSES):
            pair_b(nc.scalar.copy, g)

        acc = []
        for t in range(FIRST):
            acc.append(psum.tile([P, R], F32, name="acc%d" % t, tag="bank%d" % t))

        def multiply(t, g):
            if t < FIRST:
                w = g_first[g][:, t * P : (t + 1) * P]
            else:
                k = 0
                while t >= CHUNKS[k][1]:
                    k = k + 1
                j = t - CHUNKS[k][0]
                w = g_rest[k][:, g, j * P : (j + 1) * P]
            nc.tensor.matmul_mx(
                out=acc[t][:],
                lhsT=w.bitcast(E5M2X4),
                lhsT_scale=scales[:, g, t * P : (t + 1) * P],
                rhs=codes[g][:].bitcast(E4M3X4),
                rhs_scale=code_scales[g][:],
                start=(g == 0),
                stop=(g == PASSES - 1),
            )

        for g in range(PASSES):
            kr = work.tile([P, R, 4], BF16, name="kr", align_bytes=64)
            nc.vector.tensor_tensor(out=kr[:, 0:H, :], in0=c_by_word[:, 0:H, :], in1=b_fours[g][:], op=MULT)
            nc.vector.tensor_tensor(
                out=kr[:, H:R, :].rearrange("p r (u e) -> p r u e", e=2),
                in0=c_by_word[:, H:R, :].rearrange("p r (u e) -> p r u e", e=2),
                in1=b_pairs[g][:].unsqueeze(2).to_broadcast([P, H, 2, 2]),
                op=MULT,
            )
            for d in range(2):
                cols = slice(d * H, (d + 1) * H)
                nc.vector.quantize_mx(
                    out=codes[g][:, cols].bitcast(E4M3X4),
                    scales=code_scales[g][:, cols],
                    in_=kr[:, cols, :].rearrange("p r t -> p (r t)"),
                )
            for t in range(FIRST):
                multiply(t, g)

        ridge_part = keep.tile([P, TILES, R], F32, name="ridge_part")
        result = keep.tile([P, TILES, R], F32, name="result")

        def regularise(t):
            for n in (t, t + 1):
                nc.vector.tensor_tensor(
                    out=ridge_part[:, n, :], in0=a_sb[n // 4][:, n % 4, :], in1=wr_wide[:, 1, :], op=MULT
                )

        def weigh(t, c0=0, c1=R):
            nc.vector.tensor_tensor(out=result[:, t, c0:c1], in0=acc[t][:, c0:c1], in1=w_rep[:, c0:c1], op=MULT)

        def finish(engine, t, c0=0, c1=R):
            part = result[:, t, c0:c1]
            engine.tensor_tensor(out=part, in0=part, in1=ridge_part[:, t, c0:c1], op=ADD)
            nc.sync.dma_start(out=out_tiles[:, t, c0:c1], in_=part)

        def product(t):
            acc.append(psum.tile([P, R], F32, name="acc%d" % t, tag="bank%d" % (t % 7)))
            for g in range(PASSES):
                multiply(t, g)

        ridge_after = {1: 0, 3: 2, 5: 4, 6: 6, 7: 8, 9: 10, 10: 12, 11: 14}
        regular = 0
        finished = 0
        for t in range(14):
            weigh(t)
            if t + 7 < TILES:
                product(t + 7)
            if t in ridge_after:
                regularise(ridge_after[t])
                regular = ridge_after[t] + 2
            while finished < min(regular, t + 1, 11):
                finish(nc.gpsimd, finished)
                finished = finished + 1
        finish(nc.vector, 11)
        finish(nc.vector, 12)
        weigh(14)
        finish(nc.vector, 13)
        finish(nc.vector, 14)
        last = TILES - 1
        weigh(last, 0, H)
        weigh(last, H, R)
        finish(nc.vector, last, 0, H)
        finish(nc.vector, last, H, R)
